import numpy as np
import ml_dtypes


def mxq(x, axis, fmt="e4m3"):
    dtype, down = {"e4m3": (ml_dtypes.float8_e4m3fn, 7), "e5m2": (ml_dtypes.float8_e5m2, 14)}[fmt]
    v = np.moveaxis(np.asarray(x, np.float32).astype(ml_dtypes.bfloat16).astype(np.float64), axis, -1)
    blocks = v.reshape(v.shape[:-1] + (-1, 32))
    amax = np.abs(blocks).max(-1, keepdims=True)
    byte = np.maximum(np.where(amax > 0, np.frexp(amax)[1] - 1 + 127, 0) - down, 1)
    scale = np.exp2(byte - 127.0)
    codes = (blocks / scale).astype(np.float32).astype(dtype).astype(np.float64)
    return np.moveaxis((codes * scale).reshape(v.shape), -1, axis)


WIDE = False


def mx_kscale(k):
    if not WIDE:
        return np.ones(k)
    levels = np.array([10, -10, 5, -5, 0])
    if k % 512:
        return np.exp2(np.random.permutation(np.resize(levels, k // 32))).repeat(32)
    a = np.empty((k // 512, 16))
    for p in range(k // 512):
        a[p, :8] = np.random.permutation(np.resize(levels, 8))
        for g in range(8):
            far = levels[np.abs(levels - a[p, g]) >= 10]
            a[p, g + 8] = far[np.random.randint(len(far))]
    return np.exp2(a.ravel()).repeat(32)


def f64(x):
    return np.asarray(x).astype(np.float64)


def striped(idx):
    return np.tile(np.asarray(idx).reshape(-1, 16).T, (8, 1)).astype(np.uint16)


def unstriped(offs):
    return offs[:16].T.reshape(-1).astype(np.int64)


E2M1 = np.array([0.0, 0.5, 1.0, 1.5, 2.0, 3.0, 4.0, 6.0, -0.0, -0.5, -1.0, -1.5, -2.0, -3.0, -4.0, -6.0])


def pack_weight(w, fmt):
    k, n = w.shape
    w = f64(np.asarray(w, np.float32).astype(ml_dtypes.bfloat16)).reshape(k // 32, 32, n)
    amax = np.abs(w).max(1)
    if fmt == "e4m3":
        byte = np.frexp(amax)[1] - 1 + 127 - 7
    else:
        mant, ex = np.frexp(amax / 6.0)
        byte = np.where(mant > 0.5, ex, ex - 1) + 127
    byte = np.clip(np.where(amax > 0, byte, 1), 1, 254)
    scaled = (w * np.exp2(127.0 - byte)[:, None, :]).reshape(k, n).astype(np.float32)
    by_word = np.ascontiguousarray(scaled.reshape(k // 512, 128, 4, n).transpose(0, 1, 3, 2))
    if fmt == "e4m3":
        words = by_word.astype(ml_dtypes.float8_e4m3fn).view(np.uint8)
    else:
        c = by_word.astype(ml_dtypes.float4_e2m1fn).view(np.uint8) & 0xF
        words = (c[..., 0::2] | (c[..., 1::2] << 4)).reshape(k // 512, 128, 2 * n)
    return np.ascontiguousarray(words), np.ascontiguousarray(byte.astype(np.uint8).reshape(k // 512, 16, n))


def unpack_weight(words, scales, fmt):
    g, _, n = scales.shape
    words = np.ascontiguousarray(words).reshape(g, 128, n, -1)
    if fmt == "e4m3":
        vals = words.view(ml_dtypes.float8_e4m3fn).astype(np.float64)
    else:
        nib = np.empty((g, 128, n, 4), np.uint8)
        nib[..., 0::2] = words & 0xF
        nib[..., 1::2] = words >> 4
        vals = E2M1[nib]
    vals = vals * np.repeat(np.exp2(scales.astype(np.float64) - 127.0), 8, axis=1)[..., None]
    return vals.transpose(0, 1, 3, 2).reshape(g * 512, n)


def softplus(v):
    return np.log(1.0 + np.exp(v))


K, T, J, I, N = 512, 1024, 512, 512, 256


def setup_inputs():
    n = np.random.standard_normal
    idx = np.random.permutation(T)[:J]
    idx2 = np.random.permutation(T)[:I]
    fk = mx_kscale(K)
    wap = pack_weight(n((K, N)) * 1 / np.sqrt(K) * fk[:, None], "e4m3")
    vap = pack_weight(n((K, N)) * 1 / np.sqrt(K) * fk[:, None], "e2m1")
    wbp = pack_weight(n((K, N)) * 1 / np.sqrt(K) * fk[:, None], "e4m3")
    vbp = pack_weight(n((K, N)) * 1 / np.sqrt(K) * fk[:, None], "e2m1")
    return {
        "xt": (n((K, T)) / fk[:, None]).astype(np.float32),
        "wa_words": wap[0],
        "wa_scales": wap[1],
        "va_words": vap[0],
        "va_scales": vap[1],
        "wb_words": wbp[0],
        "wb_scales": wbp[1],
        "vb_words": vbp[0],
        "vb_scales": vbp[1],
        "pr": (np.random.uniform(0.4, 2.0, (N, T))).astype(np.float32),
        "old": (1.0 * n((N, T))).astype(np.float32),
        "offs": striped(idx),
        "offs2": striped(idx2),
    }


def reference(xt, wa_words, wa_scales, va_words, va_scales, wb_words, wb_scales, vb_words, vb_scales, pr, old, offs, offs2):
    idx = unstriped(offs)
    idx2 = unstriped(offs2)
    wau = unpack_weight(wa_words, wa_scales, "e4m3")
    vau = unpack_weight(va_words, va_scales, "e2m1")
    wbu = unpack_weight(wb_words, wb_scales, "e4m3")
    vbu = unpack_weight(vb_words, vb_scales, "e2m1")
    xtidxq = mxq(f64(xt)[:, idx], 0, "e4m3")
    a = wau.T @ xtidxq
    u = vau.T @ xtidxq
    xtidx2q = mxq(f64(xt)[:, idx2], 0, "e4m3")
    b = wbu.T @ xtidx2q
    v = vbu.T @ xtidx2q
    sa = softplus(u)
    sb = softplus(v)
    pa = sa * a
    pb = sb * b
    na = np.zeros((N, T))
    na[:, idx] = pa
    da = np.zeros((N, T))
    da[:, idx] = sa
    nb = np.zeros((N, T))
    nb[:, idx2] = pb
    db = np.zeros((N, T))
    db[:, idx2] = sb
    y = (na + nb + f64(pr) * f64(old)) / (da + db + f64(pr))
    return y

@@ -1,0 +1,255 @@
+from contextlib import ExitStack
+
+import concourse.mybir as mybir
+from concourse.masks import make_identity
+
+K, T, S, N = 512, 1024, 512, 256
+FLOPS = 4 * 2 * K * N * S
+
+F32 = mybir.dt.float32
+BF16 = mybir.dt.bfloat16
+I32 = mybir.dt.int32
+U32 = mybir.dt.uint32
+U16 = mybir.dt.uint16
+U8 = mybir.dt.uint8
+FP8X4 = mybir.dt.float8_e4m3fn_x4
+FP4X4 = mybir.dt.float4_e2m1fn_x4
+ACT = mybir.ActivationFunctionType
+ALU = mybir.AluOpType
+
+P = 128
+BANK = 512
+
+
+def tile_moe_experts_write_with_weights_kernel(
+    tc, xt, wa_words, wa_scales, va_words, va_scales, wb_words, wb_scales, vb_words, vb_scales, pr, old, offs, offs2, out
+):
+    nc = tc.nc
+    with ExitStack() as ctx:
+        sb = ctx.enter_context(tc.tile_pool(name="sb", bufs=1))
+        ps = ctx.enter_context(tc.psum_pool(name="ps", bufs=1))
+        bank = [ps.tile([P, BANK], F32, name=f"bank{i}") for i in range(8)]
+
+        planes = sb.tile([P, 4 * N], U8, name="planes", align_bytes=64)
+        nc.vector.memset(planes[:].bitcast(I32), 0)
+
+        def load_scales(slot, scales):
+            rows = scales[0].bitcast(I32)
+            for q in range(4):
+                nc.sync.dma_start(
+                    out=planes[32 * q : 32 * q + 4, slot * N : (slot + 1) * N].bitcast(I32), in_=rows[4 * q : 4 * q + 4, :]
+                )
+
+        def load_words(name, words, width):
+            tile = sb.tile([P, width], U8, name=name, align_bytes=64)
+            nc.sync.dma_start(out=tile[:].bitcast(I32), in_=words.bitcast(I32))
+            return tile
+
+        list_a = sb.tile([P, S // 16], U16, name="list_a")
+        list_b = sb.tile([P, S // 16], U16, name="list_b")
+        nc.sync.dma_start(list_a[:], offs)
+        rows_of = xt.rearrange("(p j) t -> p j t", j=4)
+        raw = {}
+        for pair in range(2):
+            for half in range(2):
+                raw[pair, half] = sb.tile([P, 2, T // 2], F32, name=f"raw{pair}{half}")
+                nc.sync.dma_start(
+                    out=raw[pair, half][:], in_=rows_of[:, 2 * pair : 2 * pair + 2, half * (T // 2) : (half + 1) * (T // 2)]
+                )
+        va = load_words("va", va_words[0], 2 * N)
+        load_scales(0, va_scales)
+        nc.sync.dma_start(list_b[:], offs2)
+        vb = load_words("vb", vb_words[0], 2 * N)
+        load_scales(1, vb_scales)
+        prior = sb.tile([P, 2, T], F32, name="prior")
+        state = sb.tile([P, 2, T], F32, name="state")
+        nc.sync.dma_start(out=prior[:], in_=pr.rearrange("(h p) t -> p h t", p=P))
+        nc.sync.dma_start(out=state[:], in_=old.rearrange("(h p) t -> p h t", p=P))
+        wa = load_words("wa", wa_words[0].rearrange("p n r -> p (n r)"), 4 * N)
+        load_scales(2, wa_scales)
+        wb = load_words("wb", wb_words[0].rearrange("p n r -> p (n r)"), 4 * N)
+        load_scales(3, wb_scales)
+
+        ident = sb.tile([P, P], F32, name="ident")
+        make_identity(nc, ident[:])
+
+        pairs = [sb.tile([P, T], U32, name=f"pairs{i}") for i in range(2)]
+
+        def cast(pair, half, copy):
+            cols = slice(half * (T // 2), (half + 1) * (T // 2))
+            copy(
+                out=pairs[pair][:, cols].bitcast(BF16).rearrange("p (t j) -> p t j", j=2),
+                in_=raw[pair, half][:].rearrange("p j t -> p t j"),
+            )
+
+        picked = {}
+        lists = [list_a, list_b]
+
+        def gather(e, pair):
+            if pair == 0:
+                picked[e] = sb.tile([P, 2, S], U32, name=f"picked{e}", tag=f"stage{2 * e}", align_bytes=64)
+            nc.vector.tensor_copy(picked[e][:, pair, :], pairs[pair][:].indirect(lists[e][:]))
+
+        def quantise(e):
+            grouped = sb.tile([P, 4 * S], BF16, name=f"grouped{e}", tag=f"stage{2 + e}", align_bytes=64)
+            nc.vector.tensor_copy(
+                out=grouped[:].bitcast(I32).rearrange("p (c w) -> p c w", w=2),
+                in_=picked[e][:].bitcast(I32).rearrange("p w c -> p c w"),
+            )
+            codes = sb.tile([P, S], U32, name=f"codes{e}", align_bytes=64)
+            scale = sb.tile([P, S], U8, name=f"scale{e}", align_bytes=64)
+            nc.vector.quantize_mx(out=codes[:].bitcast(FP8X4), scales=scale[:], in_=grouped[:])
+            return codes, scale
+
+        def product(acc, words, dtype, slot, h, tokens):
+            width = P * (2 if dtype == FP4X4 else 4)
+            nc.tensor.matmul_mx(
+                out=acc[:],
+                lhsT=words[:, h * width : (h + 1) * width].bitcast(dtype),
+                lhsT_scale=planes[:, slot * N + h * P : slot * N + (h + 1) * P],
+                rhs=tokens[0][:].bitcast(FP8X4),
+                rhs_scale=tokens[1][:],
+                start=True,
+                stop=True,
+            )
+
+        def turn(banks, src, first, last):
+            for j in range(T // P):
+                nc.tensor.matmul(
+                    banks[j // 4][:, (j % 4) * P : (j % 4 + 1) * P],
+                    lhsT=src[:, j * P : (j + 1) * P],
+                    rhs=ident[:],
+                    start=first and j % 4 == 0,
+                    stop=last and j % 4 == 3,
+                    is_transpose=True,
+                )
+
+        ping = sb.tile([P, 2, S], F32, name="ping")
+        pong = sb.tile([P, 2, S], F32, name="pong")
+
+        def log_part(e, accs, mag, decay):
+            for h in range(2):
+                nc.scalar.activation(mag[:, h, :], accs[h][:], ACT.Abs)
+            nc.scalar.activation(decay[:], mag[:], ACT.Exp, scale=-1.0)
+            logs = [sb.tile([P, S], F32, name=f"log{e}{h}") for h in range(2)]
+            for h in range(2):
+                nc.scalar.activation(logs[h][:], decay[:, h, :], ACT.Ln, bias=1.0)
+            return logs
+
+        def softplus(name, acc, log):
+            w = sb.tile([P, S], F32, name=name)
+            nc.vector.scalar_tensor_tensor(w[:], acc[:], 0.0, log[:], ALU.max, ALU.add)
+            return w
+
+        def evacuate(v, acc):
+            nc.scalar.copy(v[:], acc[:])
+            return v
+
+        cast(0, 0, nc.scalar.copy)
+        cast(0, 1, nc.vector.tensor_copy)
+        gather(0, 0)
+        cast(1, 0, nc.scalar.copy)
+        cast(1, 1, nc.vector.tensor_copy)
+        gather(0, 1)
+        tok_a = quantise(0)
+        for h in range(2):
+            product(bank[h], va, FP4X4, 0, h, tok_a)
+        log_a = log_part(0, bank[0:2], ping, pong)
+        gather(1, 0)
+        gather(1, 1)
+        tok_b = quantise(1)
+        for h in range(2):
+            product(bank[3 + h], vb, FP4X4, 1, h, tok_b)
+        product(bank[2], wa, FP8X4, 2, 0, tok_a)
+        product(bank[5], wb, FP8X4, 3, 0, tok_b)
+        product(bank[6], wa, FP8X4, 2, 1, tok_a)
+        product(bank[7], wb, FP8X4, 3, 1, tok_b)
+
+        win = {}
+        for name in ("da0", "da1", "na0", "db0", "db1", "nb0", "na1", "nb1"):
+            win[name] = sb.tile([P, T], F32, name=name)
+            nc.vector.memset(win[name][:], 0.0)
+
+        kept = sb.tile([P, 2, T], F32, name="kept", tag="stage3", align_bytes=64)
+        for h in range(2):
+            nc.vector.tensor_tensor(kept[:, h, :], prior[:, h, :], state[:, h, :], ALU.mult)
+
+        sa0 = softplus("sa0", bank[0], log_a[0])
+        nc.vector.tensor_copy(win["da0"][:].indirect(list_a[:]), sa0[:])
+        sa1 = softplus("sa1", bank[1], log_a[1])
+        nc.vector.tensor_copy(win["da1"][:].indirect(list_a[:]), sa1[:])
+        a0 = evacuate(log_a[0], bank[2])
+        nc.vector.tensor_tensor(win["na0"][:].indirect(list_a[:]), sa0[:], a0[:], ALU.mult)
+
+        log_b = log_part(1, bank[3:5], pong, ping)
+        b0 = evacuate(log_a[1], bank[5])
+        sb0 = softplus("sb0", bank[3], log_b[0])
+        sb1 = softplus("sb1", bank[4], log_b[1])
+        nc.vector.tensor_copy(win["db0"][:].indirect(list_b[:]), sb0[:])
+        nc.vector.tensor_copy(win["db1"][:].indirect(list_b[:]), sb1[:])
+        nc.vector.tensor_tensor(win["nb0"][:].indirect(list_b[:]), sb0[:], b0[:], ALU.mult)
+        a1 = evacuate(log_b[1], bank[6])
+        nc.vector.tensor_tensor(win["na1"][:].indirect(list_a[:]), sa1[:], a1[:], ALU.mult)
+
+        den_banks = [[bank[2], bank[5]], [bank[0], bank[1]]]
+        log_den = sb.tile([P, 2 * T], F32, name="log_den")
+        for h in range(2):
+            turn(den_banks[h], prior[:, h, :], True, False)
+            turn(den_banks[h], win[f"da{h}"], False, False)
+            turn(den_banks[h], win[f"db{h}"], False, True)
+            for i in range(2):
+                at = h * T + i * BANK
+                nc.scalar.activation(log_den[:, at : at + BANK], den_banks[h][i][:], ACT.Ln)
+        inv = sb.tile([P, 2 * T], F32, name="inv")
+        nc.scalar.activation(inv[:], log_den[:], ACT.Exp, scale=-1.0)
+        b1 = log_den[:, :S]
+        nc.scalar.copy(b1, bank[7][:])
+
+        num0 = [bank[3], bank[4]]
+        turn(num0, kept[:, 0, :], True, False)
+        turn(num0, win["na0"], False, False)
+        turn(num0, win["nb0"], False, True)
+        y0t = sb.tile([P, T], F32, name="y0t")
+        for i in range(2):
+            cols = slice(i * BANK, (i + 1) * BANK)
+            nc.vector.tensor_tensor(y0t[:, cols], num0[i][:], inv[:, cols], ALU.mult)
+        nc.vector.tensor_tensor(win["nb1"][:].indirect(list_b[:]), sb1[:], b1, ALU.mult)
+
+        rest_t = [bank[6], bank[2]]
+        turn(rest_t, kept[:, 1, :], True, False)
+        turn(rest_t, win["na1"], False, True)
+        inv1 = [bank[0], bank[1]]
+        turn(inv1, inv[:, T:], True, True)
+        rest_sb = log_den[:, T:]
+        for i in range(2):
+            nc.scalar.copy(rest_sb[:, i * BANK : (i + 1) * BANK], rest_t[i][:])
+        rest = [bank[5], bank[7]]
+        turn(rest, rest_sb, True, True)
+
+        turn(num0, y0t, True, True)
+        y0 = sb.tile([P, T], F32, name="y0")
+        for i in range(2):
+            cols = slice(i * BANK, (i + 1) * BANK)
+            nc.scalar.copy(y0[:, cols], num0[i][:])
+            nc.sync.dma_start(out=out[0:P, cols], in_=y0[:, cols])
+
+        num1 = sb.tile([P, T], F32, name="num1")
+        y1 = sb.tile([P, T], F32, name="y1")
+        step = 256
+
+        def add(c):
+            i, lo = divmod(c * step, BANK)
+            cols = slice(c * step, (c + 1) * step)
+            nc.vector.tensor_tensor(num1[:, cols], rest[i][:, lo : lo + step], win["nb1"][:, cols], ALU.add)
+
+        def finish(c):
+            i, lo = divmod(c * step, BANK)
+            cols = slice(c * step, (c + 1) * step)
+            nc.vector.tensor_tensor(y1[:, cols], inv1[i][:, lo : lo + step], num1[:, cols], ALU.mult)
+            nc.sync.dma_start(out=out[P : 2 * P, cols], in_=y1[:, cols])
+
+        add(0)
+        for c in range(1, T // step):
+            add(c)
+            finish(c - 1)
+        finish(T // step - 1)

@@ -48,6 +48,7 @@ def tile_moe_experts_write_with_weights_kernel(
         list_a = sb.tile([P, S // 16], U16, name="list_a")
         list_b = sb.tile([P, S // 16], U16, name="list_b")
         nc.sync.dma_start(list_a[:], offs)
+        nc.sync.dma_start(list_b[:], offs2)
         rows_of = xt.rearrange("(p j) t -> p j t", j=4)
         raw = {}
         for pair in range(2):
@@ -58,47 +59,47 @@ def tile_moe_experts_write_with_weights_kernel(
                 )
         va = load_words("va", va_words[0], 2 * N)
         load_scales(0, va_scales)
-        nc.sync.dma_start(list_b[:], offs2)
+        wa = load_words("wa", wa_words[0].rearrange("p n r -> p (n r)"), 4 * N)
+        load_scales(2, wa_scales)
         vb = load_words("vb", vb_words[0], 2 * N)
         load_scales(1, vb_scales)
+        wb = load_words("wb", wb_words[0].rearrange("p n r -> p (n r)"), 4 * N)
+        load_scales(3, wb_scales)
         prior = sb.tile([P, 2, T], F32, name="prior")
         state = sb.tile([P, 2, T], F32, name="state")
         nc.sync.dma_start(out=prior[:], in_=pr.rearrange("(h p) t -> p h t", p=P))
         nc.sync.dma_start(out=state[:], in_=old.rearrange("(h p) t -> p h t", p=P))
-        wa = load_words("wa", wa_words[0].rearrange("p n r -> p (n r)"), 4 * N)
-        load_scales(2, wa_scales)
-        wb = load_words("wb", wb_words[0].rearrange("p n r -> p (n r)"), 4 * N)
-        load_scales(3, wb_scales)
 
         ident = sb.tile([P, P], F32, name="ident")
         make_identity(nc, ident[:])
 
         pairs = [sb.tile([P, T], U32, name=f"pairs{i}") for i in range(2)]
 
-        def cast(pair, half, copy):
-            cols = slice(half * (T // 2), (half + 1) * (T // 2))
+        def cast(pair, half, copy, lo=0, hi=T // 2):
+            first = half * (T // 2)
             copy(
-                out=pairs[pair][:, cols].bitcast(BF16).rearrange("p (t j) -> p t j", j=2),
-                in_=raw[pair, half][:].rearrange("p j t -> p t j"),
+                out=pairs[pair][:, first + lo : first + hi].bitcast(BF16).rearrange("p (t j) -> p t j", j=2),
+                in_=raw[pair, half][:, :, lo:hi].rearrange("p j t -> p t j"),
             )
 
-        picked = {}
+        stage = sb.tile([P, 2 * S], U32, name="stage", align_bytes=64)
+        picked_a = sb.tile([P, 2 * S], U32, name="picked_a")
+        grouped_b = sb.tile([P, 2 * S], U32, name="grouped_b", align_bytes=64)
+        picked = [picked_a[:], stage[:]]
+        woven = [stage[:], grouped_b[:]]
         lists = [list_a, list_b]
 
         def gather(e, pair):
-            if pair == 0:
-                picked[e] = sb.tile([P, 2, S], U32, name=f"picked{e}", tag=f"stage{2 * e}", align_bytes=64)
-            nc.vector.tensor_copy(picked[e][:, pair, :], pairs[pair][:].indirect(lists[e][:]))
+            nc.vector.tensor_copy(picked[e][:, pair * S : (pair + 1) * S], pairs[pair][:].indirect(lists[e][:]))
 
         def quantise(e):
-            grouped = sb.tile([P, 4 * S], BF16, name=f"grouped{e}", tag=f"stage{2 + e}", align_bytes=64)
             nc.vector.tensor_copy(
-                out=grouped[:].bitcast(I32).rearrange("p (c w) -> p c w", w=2),
-                in_=picked[e][:].bitcast(I32).rearrange("p w c -> p c w"),
+                out=woven[e].bitcast(I32).rearrange("p (c w) -> p c w", w=2),
+                in_=picked[e].bitcast(I32).rearrange("p (w c) -> p c w", w=2),
             )
             codes = sb.tile([P, S], U32, name=f"codes{e}", align_bytes=64)
             scale = sb.tile([P, S], U8, name=f"scale{e}", align_bytes=64)
-            nc.vector.quantize_mx(out=codes[:].bitcast(FP8X4), scales=scale[:], in_=grouped[:])
+            nc.vector.quantize_mx(out=codes[:].bitcast(FP8X4), scales=scale[:], in_=woven[e].bitcast(BF16))
             return codes, scale
 
         def product(acc, words, dtype, slot, h, tokens):
@@ -124,101 +125,112 @@ def tile_moe_experts_write_with_weights_kernel(
                     is_transpose=True,
                 )
 
-        ping = sb.tile([P, 2, S], F32, name="ping")
-        pong = sb.tile([P, 2, S], F32, name="pong")
+        tiny = 2.0**-64
+        gates = sb.tile([P, 5 * S], F32, name="gates")
+        logs = sb.tile([P, 5 * S], F32, name="logs")
+        log_a0 = sb.tile([P, S], F32, name="log_a0")
 
-        def log_part(e, accs, mag, decay):
-            for h in range(2):
-                nc.scalar.activation(mag[:, h, :], accs[h][:], ACT.Abs)
-            nc.scalar.activation(decay[:], mag[:], ACT.Exp, scale=-1.0)
-            logs = [sb.tile([P, S], F32, name=f"log{e}{h}") for h in range(2)]
-            for h in range(2):
-                nc.scalar.activation(logs[h][:], decay[:, h, :], ACT.Ln, bias=1.0)
-            return logs
-
-        def softplus(name, acc, log):
-            w = sb.tile([P, S], F32, name=name)
-            nc.vector.scalar_tensor_tensor(w[:], acc[:], 0.0, log[:], ALU.max, ALU.add)
+        def softplus(w, acc, log):
+            nc.vector.scalar_tensor_tensor(w, log, -1.0, acc[:], ALU.mult, ALU.max)
             return w
 
         def evacuate(v, acc):
-            nc.scalar.copy(v[:], acc[:])
+            nc.scalar.copy(v, acc[:])
             return v
 
+        share = 352
         cast(0, 0, nc.scalar.copy)
         cast(0, 1, nc.vector.tensor_copy)
         gather(0, 0)
         cast(1, 0, nc.scalar.copy)
-        cast(1, 1, nc.vector.tensor_copy)
+        cast(1, 1, nc.vector.tensor_copy, 0, share)
+        cast(1, 1, nc.scalar.copy, share, T // 2)
         gather(0, 1)
         tok_a = quantise(0)
         for h in range(2):
             product(bank[h], va, FP4X4, 0, h, tok_a)
-        log_a = log_part(0, bank[0:2], ping, pong)
+        spread = gates[:, : 4 * S].rearrange("p (a b) -> p a b", a=4)[:, :, :P]
+        nc.scalar.activation(spread, bank[0][:].rearrange("p (a b) -> p a b", a=4), ACT.Sigmoid, scale=-1.0)
+        nc.scalar.activation(log_a0[:].rearrange("p (a b) -> p a b", a=4), spread, ACT.Ln, bias=tiny)
         gather(1, 0)
         gather(1, 1)
         tok_b = quantise(1)
         for h in range(2):
             product(bank[3 + h], vb, FP4X4, 1, h, tok_b)
         product(bank[2], wa, FP8X4, 2, 0, tok_a)
-        product(bank[5], wb, FP8X4, 3, 0, tok_b)
         product(bank[6], wa, FP8X4, 2, 1, tok_a)
+        product(bank[5], wb, FP8X4, 3, 0, tok_b)
         product(bank[7], wb, FP8X4, 3, 1, tok_b)
 
         win = {}
-        for name in ("da0", "da1", "na0", "db0", "db1", "nb0", "na1", "nb1"):
-            win[name] = sb.tile([P, T], F32, name=name)
-            nc.vector.memset(win[name][:], 0.0)
+        for name in ("a0", "a1", "a2", "b0", "b1"):
+            win[name] = sb.tile([P, T], F32, name=f"win_{name}")
+            (nc.vector if name in ("a0", "a1", "a2") else nc.gpsimd).memset(win[name][:], 0.0)
 
-        kept = sb.tile([P, 2, T], F32, name="kept", tag="stage3", align_bytes=64)
+        den_banks = [[bank[1], bank[5]], [bank[0], bank[2]]]
+        sa0_tile = sb.tile([P, S], F32, name="sa0", tag="sa0")
+        sa0 = softplus(sa0_tile[:], bank[0], log_a0[:])
+        nc.vector.tensor_copy(win["a0"][:].indirect(list_a[:]), sa0)
+        a0 = evacuate(gates[:, 3 * S : 4 * S], bank[2])
+        nc.vector.tensor_tensor(win["a1"][:].indirect(list_a[:]), sa0, a0, ALU.mult)
+
+        kept = sb.tile([P, 2, T], F32, name="kept", tag="sa0")
         for h in range(2):
-            nc.vector.tensor_tensor(kept[:, h, :], prior[:, h, :], state[:, h, :], ALU.mult)
+            for i in range(2):
+                cols = slice(i * BANK, (i + 1) * BANK)
+                nc.gpsimd.tensor_tensor(kept[:, h, cols], prior[:, h, cols], state[:, h, cols], ALU.mult)
 
-        sa0 = softplus("sa0", bank[0], log_a[0])
-        nc.vector.tensor_copy(win["da0"][:].indirect(list_a[:]), sa0[:])
-        sa1 = softplus("sa1", bank[1], log_a[1])
-        nc.vector.tensor_copy(win["da1"][:].indirect(list_a[:]), sa1[:])
-        a0 = evacuate(log_a[0], bank[2])
-        nc.vector.tensor_tensor(win["na0"][:].indirect(list_a[:]), sa0[:], a0[:], ALU.mult)
-
-        log_b = log_part(1, bank[3:5], pong, ping)
-        b0 = evacuate(log_a[1], bank[5])
-        sb0 = softplus("sb0", bank[3], log_b[0])
-        sb1 = softplus("sb1", bank[4], log_b[1])
-        nc.vector.tensor_copy(win["db0"][:].indirect(list_b[:]), sb0[:])
-        nc.vector.tensor_copy(win["db1"][:].indirect(list_b[:]), sb1[:])
-        nc.vector.tensor_tensor(win["nb0"][:].indirect(list_b[:]), sb0[:], b0[:], ALU.mult)
-        a1 = evacuate(log_b[1], bank[6])
-        nc.vector.tensor_tensor(win["na1"][:].indirect(list_a[:]), sa1[:], a1[:], ALU.mult)
-
-        den_banks = [[bank[2], bank[5]], [bank[0], bank[1]]]
+        for slot, acc in ((1, bank[1]), (0, bank[3]), (2, bank[4])):
+            nc.scalar.activation(gates[:, slot * S : (slot + 1) * S], acc[:], ACT.Sigmoid, scale=-1.0)
+        lo, hi = S - 64, 2 * S + 64
+        nc.scalar.activation(logs[:, lo:hi], gates[:, lo:hi], ACT.Ln, bias=tiny)
+        nc.scalar.activation(
+            logs[:, : 2 * hi].rearrange("p (a b) -> p a b", a=2)[:, :, :lo],
+            gates[:, : 2 * hi].rearrange("p (a b) -> p a b", a=2)[:, :, :lo],
+            ACT.Ln,
+            bias=tiny,
+        )
+        sa1 = softplus(a0, bank[1], logs[:, S : 2 * S])
+        nc.vector.tensor_copy(win["a2"][:].indirect(list_a[:]), sa1)
+        b0 = evacuate(logs[:, S : 2 * S], bank[5])
+        turn(den_banks[0], win["a0"], True, False)
+        turn(den_banks[1], win["a2"], True, False)
+        for h in range(2):
+            turn(den_banks[h], prior[:, h, :], False, False)
+        weights_b = sb.tile([P, 2, S], F32, name="weights_b")
+        sb0 = softplus(weights_b[:, 0, :], bank[3], logs[:, :S])
+        sb1 = softplus(weights_b[:, 1, :], bank[4], logs[:, 2 * S : 3 * S])
+        nc.vector.tensor_copy(win["b0"][:].indirect(list_b[:]), sb0)
+        nc.vector.tensor_copy(win["b1"][:].indirect(list_b[:]), sb1)
         log_den = sb.tile([P, 2 * T], F32, name="log_den")
         for h in range(2):
-            turn(den_banks[h], prior[:, h, :], True, False)
-            turn(den_banks[h], win[f"da{h}"], False, False)
-            turn(den_banks[h], win[f"db{h}"], False, True)
+            turn(den_banks[h], win[f"b{h}"], False, True)
             for i in range(2):
                 at = h * T + i * BANK
                 nc.scalar.activation(log_den[:, at : at + BANK], den_banks[h][i][:], ACT.Ln)
+        num0 = [bank[3], bank[4]]
+        turn(num0, win["a1"], True, False)
+        turn(num0, kept[:, 0, :], False, False)
+        nc.vector.tensor_tensor(win["b0"][:].indirect(list_b[:]), sb0, b0, ALU.mult)
+        a1 = evacuate(logs[:, 2 * S : 3 * S], bank[6])
+        nc.vector.tensor_tensor(win["a0"][:].indirect(list_a[:]), sa1, a1, ALU.mult)
+
         inv = sb.tile([P, 2 * T], F32, name="inv")
         nc.scalar.activation(inv[:], log_den[:], ACT.Exp, scale=-1.0)
         b1 = log_den[:, :S]
         nc.scalar.copy(b1, bank[7][:])
 
-        num0 = [bank[3], bank[4]]
-        turn(num0, kept[:, 0, :], True, False)
-        turn(num0, win["na0"], False, False)
-        turn(num0, win["nb0"], False, True)
+        turn(num0, win["b0"], False, True)
         y0t = sb.tile([P, T], F32, name="y0t")
         for i in range(2):
             cols = slice(i * BANK, (i + 1) * BANK)
             nc.vector.tensor_tensor(y0t[:, cols], num0[i][:], inv[:, cols], ALU.mult)
-        nc.vector.tensor_tensor(win["nb1"][:].indirect(list_b[:]), sb1[:], b1, ALU.mult)
+        nc.vector.tensor_tensor(win["b1"][:].indirect(list_b[:]), sb1, b1, ALU.mult)
 
-        rest_t = [bank[6], bank[2]]
+        rest_t = [bank[6], bank[1]]
         turn(rest_t, kept[:, 1, :], True, False)
-        turn(rest_t, win["na1"], False, True)
-        inv1 = [bank[0], bank[1]]
+        turn(rest_t, win["a0"], False, True)
+        inv1 = [bank[0], bank[2]]
         turn(inv1, inv[:, T:], True, True)
         rest_sb = log_den[:, T:]
         for i in range(2):
@@ -240,7 +252,7 @@ def tile_moe_experts_write_with_weights_kernel(
         def add(c):
             i, lo = divmod(c * step, BANK)
             cols = slice(c * step, (c + 1) * step)
-            nc.vector.tensor_tensor(num1[:, cols], rest[i][:, lo : lo + step], win["nb1"][:, cols], ALU.add)
+            nc.vector.tensor_tensor(num1[:, cols], rest[i][:, lo : lo + step], win["b1"][:, cols], ALU.add)
 
         def finish(c):
             i, lo = divmod(c * step, BANK)

@@ -47,8 +47,6 @@ def tile_moe_experts_write_with_weights_kernel(
 
         list_a = sb.tile([P, S // 16], U16, name="list_a")
         list_b = sb.tile([P, S // 16], U16, name="list_b")
-        nc.sync.dma_start(list_a[:], offs)
-        nc.sync.dma_start(list_b[:], offs2)
         rows_of = xt.rearrange("(p j) t -> p j t", j=4)
         raw = {}
         for pair in range(2):
@@ -57,8 +55,11 @@ def tile_moe_experts_write_with_weights_kernel(
                 nc.sync.dma_start(
                     out=raw[pair, half][:], in_=rows_of[:, 2 * pair : 2 * pair + 2, half * (T // 2) : (half + 1) * (T // 2)]
                 )
+            if pair == 0:
+                nc.sync.dma_start(list_a[:], offs)
         va = load_words("va", va_words[0], 2 * N)
         load_scales(0, va_scales)
+        nc.sync.dma_start(list_b[:], offs2)
         wa = load_words("wa", wa_words[0].rearrange("p n r -> p (n r)"), 4 * N)
         load_scales(2, wa_scales)
         vb = load_words("vb", vb_words[0], 2 * N)
@@ -114,16 +115,21 @@ def tile_moe_experts_write_with_weights_kernel(
                 stop=True,
             )
 
-        def turn(banks, src, first, last):
-            for j in range(T // P):
+        def turn(bank_tile, at, src, start, stop):
+            blocks = src.shape[1] // P
+            for j in range(blocks):
                 nc.tensor.matmul(
-                    banks[j // 4][:, (j % 4) * P : (j % 4 + 1) * P],
+                    bank_tile[:, at + j * P : at + (j + 1) * P],
                     lhsT=src[:, j * P : (j + 1) * P],
                     rhs=ident[:],
-                    start=first and j % 4 == 0,
-                    stop=last and j % 4 == 3,
+                    start=start and j == 0,
+                    stop=stop and j == blocks - 1,
                     is_transpose=True,
                 )
+
+        def turn_wide(banks, src, start, stop):
+            for i, lo in enumerate(range(0, src.shape[1], BANK)):
+                turn(banks[i], 0, src[:, lo : min(lo + BANK, src.shape[1])], start, stop)
 
         tiny = 2.0**-64
         gates = sb.tile([P, 5 * S], F32, name="gates")
@@ -167,7 +173,6 @@ def tile_moe_experts_write_with_weights_kernel(
             win[name] = sb.tile([P, T], F32, name=f"win_{name}")
             (nc.vector if name in ("a0", "a1", "a2") else nc.gpsimd).memset(win[name][:], 0.0)
 
-        den_banks = [[bank[1], bank[5]], [bank[0], bank[2]]]
         sa0_tile = sb.tile([P, S], F32, name="sa0", tag="sa0")
         sa0 = softplus(sa0_tile[:], bank[0], log_a0[:])
         nc.vector.tensor_copy(win["a0"][:].indirect(list_a[:]), sa0)
@@ -193,66 +198,96 @@ def tile_moe_experts_write_with_weights_kernel(
         sa1 = softplus(a0, bank[1], logs[:, S : 2 * S])
         nc.vector.tensor_copy(win["a2"][:].indirect(list_a[:]), sa1)
         b0 = evacuate(logs[:, S : 2 * S], bank[5])
-        turn(den_banks[0], win["a0"], True, False)
-        turn(den_banks[1], win["a2"], True, False)
-        for h in range(2):
-            turn(den_banks[h], prior[:, h, :], False, False)
+        a1 = evacuate(gates[:, :S], bank[6])
+        b1 = evacuate(gates[:, 2 * S : 3 * S], bank[7])
         weights_b = sb.tile([P, 2, S], F32, name="weights_b")
         sb0 = softplus(weights_b[:, 0, :], bank[3], logs[:, :S])
         sb1 = softplus(weights_b[:, 1, :], bank[4], logs[:, 2 * S : 3 * S])
+        pa1 = sb.tile([P, S], F32, name="pa1")
+        pb1 = sb.tile([P, S], F32, name="pb1")
+        nc.gpsimd.tensor_tensor(pa1[:], sa1, a1, ALU.mult)
+        nc.gpsimd.tensor_tensor(pb1[:], sb1, b1, ALU.mult)
         nc.vector.tensor_copy(win["b0"][:].indirect(list_b[:]), sb0)
         nc.vector.tensor_copy(win["b1"][:].indirect(list_b[:]), sb1)
-        log_den = sb.tile([P, 2 * T], F32, name="log_den")
-        for h in range(2):
-            turn(den_banks[h], win[f"b{h}"], False, True)
-            for i in range(2):
-                at = h * T + i * BANK
-                nc.scalar.activation(log_den[:, at : at + BANK], den_banks[h][i][:], ACT.Ln)
+
+        den0, den1 = [bank[1], bank[5]], [bank[6], bank[7]]
+        last = T - P
+        turn_wide(den0, win["a0"][:], True, False)
+        turn_wide(den0, prior[:, 0, :], False, False)
+        turn_wide(den1, prior[:, 1, :], True, False)
+        turn_wide(den1, win["a2"][:, :last], False, False)
+        turn_wide(den0, win["b0"][:], False, True)
+        turn(den1[0], 0, win["b1"][:, :BANK], False, True)
+        turn(den1[1], 0, win["b1"][:, BANK:], False, False)
+        turn(den1[1], BANK - P, win["a2"][:, last:], False, True)
+        lo, hi = BANK - 64, 3 * BANK + 64
+        log_den = sb.tile([P, 2 * hi], F32, name="log_den")
+        inv = sb.tile([P, 2 * hi], F32, name="inv")
+        for slot, acc in ((1, den0[0]), (2, den0[1]), (0, den1[0]), (3, den1[1])):
+            nc.scalar.activation(log_den[:, slot * BANK : (slot + 1) * BANK], acc[:], ACT.Ln)
+
         num0 = [bank[3], bank[4]]
-        turn(num0, win["a1"], True, False)
-        turn(num0, kept[:, 0, :], False, False)
+        turn_wide(num0, win["a1"][:], True, False)
+        turn_wide(num0, kept[:, 0, :], False, False)
         nc.vector.tensor_tensor(win["b0"][:].indirect(list_b[:]), sb0, b0, ALU.mult)
-        a1 = evacuate(logs[:, 2 * S : 3 * S], bank[6])
-        nc.vector.tensor_tensor(win["a0"][:].indirect(list_a[:]), sa1, a1, ALU.mult)
+        turn_wide(num0, win["b0"][:], False, True)
+        nc.vector.tensor_copy(win["b1"][:].indirect(list_b[:]), pb1[:])
+        nc.vector.tensor_copy(win["a2"][:].indirect(list_a[:]), pa1[:])
 
-        inv = sb.tile([P, 2 * T], F32, name="inv")
-        nc.scalar.activation(inv[:], log_den[:], ACT.Exp, scale=-1.0)
-        b1 = log_den[:, :S]
-        nc.scalar.copy(b1, bank[7][:])
-
-        turn(num0, win["b0"], False, True)
+        nc.scalar.activation(inv[:, lo:hi], log_den[:, lo:hi], ACT.Exp, scale=-1.0)
+        num0_t = log_den[:, BANK : 3 * BANK]
+        inv0_t = inv[:, BANK : 3 * BANK]
         y0t = sb.tile([P, T], F32, name="y0t")
-        for i in range(2):
-            cols = slice(i * BANK, (i + 1) * BANK)
-            nc.vector.tensor_tensor(y0t[:, cols], num0[i][:], inv[:, cols], ALU.mult)
-        nc.vector.tensor_tensor(win["b1"][:].indirect(list_b[:]), sb1, b1, ALU.mult)
+        halves = [slice(0, BANK), slice(BANK, T)]
+        nc.scalar.copy(num0_t[:, halves[0]], num0[0][:])
+        nc.scalar.activation(
+            inv[:].rearrange("p (a b) -> p a b", a=2)[:, :, :lo],
+            log_den[:].rearrange("p (a b) -> p a b", a=2)[:, :, :lo],
+            ACT.Exp,
+            scale=-1.0,
+        )
+        nc.scalar.copy(num0_t[:, halves[1]], num0[1][:])
+        for cols in halves:
+            nc.gpsimd.tensor_tensor(y0t[:, cols], num0_t[:, cols], inv0_t[:, cols], ALU.mult)
 
-        rest_t = [bank[6], bank[1]]
-        turn(rest_t, kept[:, 1, :], True, False)
-        turn(rest_t, win["a0"], False, True)
-        inv1 = [bank[0], bank[2]]
-        turn(inv1, inv[:, T:], True, True)
-        rest_sb = log_den[:, T:]
-        for i in range(2):
-            nc.scalar.copy(rest_sb[:, i * BANK : (i + 1) * BANK], rest_t[i][:])
-        rest = [bank[5], bank[7]]
-        turn(rest, rest_sb, True, True)
-
-        turn(num0, y0t, True, True)
-        y0 = sb.tile([P, T], F32, name="y0")
-        for i in range(2):
-            cols = slice(i * BANK, (i + 1) * BANK)
-            nc.scalar.copy(y0[:, cols], num0[i][:])
-            nc.sync.dma_start(out=out[0:P, cols], in_=y0[:, cols])
-
-        num1 = sb.tile([P, T], F32, name="num1")
-        y1 = sb.tile([P, T], F32, name="y1")
         step = 256
+        mine = T - step
+        rest_t = [bank[0], bank[2]]
+        turn_wide(rest_t, kept[:, 1, :mine], True, False)
+        turn_wide(rest_t, win["b1"][:, :mine], False, True)
+        inv1 = den1
+        turn(inv1[0], 0, inv[:, :BANK], True, True)
+        turn(inv1[1], 0, inv[:, 3 * BANK : 4 * BANK], True, True)
+        rest_lo = log_den[:, :BANK]
+        rest_hi = log_den[:, 3 * BANK + step : 4 * BANK]
+        nc.scalar.copy(rest_lo, rest_t[0][:])
+        nc.scalar.copy(rest_hi, rest_t[1][:, : mine - BANK])
+        rest = den0
+        turn(rest[0], 0, rest_lo, True, True)
+        turn(rest[1], 0, rest_hi, True, True)
+        inv_end = sb.tile([P, step], F32, name="inv_end")
+        nc.scalar.copy(inv_end[:], inv1[1][:, BANK - step :])
+        num1 = sb.tile([P, mine], F32, name="num1")
+        rest_end = num0_t[:, :step]
+        nc.gpsimd.tensor_tensor(rest_end, kept[:, 1, mine:], win["b1"][:, mine:], ALU.add)
+
+        turn_wide(num0, y0t[:], True, True)
+        y0 = sb.tile([P, T], F32, name="y0")
+        for i, cols in enumerate(halves):
+            nc.scalar.copy(y0[:, cols], num0[i][:])
+            nc.scalar.dma_start(out=out[0:P, cols], in_=y0[:, cols])
+
+        y1 = sb.tile([P, mine], F32, name="y1")
+        num_end = num0_t[:, mine:]
+        nc.gpsimd.tensor_tensor(num_end, rest_end, win["a2"][:, mine:], ALU.add)
+        y1_end = y0t[:, mine:]
+        nc.gpsimd.tensor_tensor(y1_end, num_end, inv_end[:], ALU.mult)
+        nc.scalar.dma_start(out=out[P : 2 * P, mine:], in_=y1_end)
 
         def add(c):
             i, lo = divmod(c * step, BANK)
             cols = slice(c * step, (c + 1) * step)
-            nc.vector.tensor_tensor(num1[:, cols], rest[i][:, lo : lo + step], win["b1"][:, cols], ALU.add)
+            nc.vector.tensor_tensor(num1[:, cols], rest[i][:, lo : lo + step], win["a2"][:, cols], ALU.add)
 
         def finish(c):
             i, lo = divmod(c * step, BANK)
@@ -261,7 +296,7 @@ def tile_moe_experts_write_with_weights_kernel(
             nc.sync.dma_start(out=out[P : 2 * P, cols], in_=y1[:, cols])
 
         add(0)
-        for c in range(1, T // step):
+        for c in range(1, mine // step):
             add(c)
             finish(c - 1)
-        finish(T // step - 1)
+        finish(mine // step - 1)

from contextlib import ExitStack

import concourse.mybir as mybir
from concourse.masks import make_identity

K, T, S, N = 512, 1024, 512, 256
FLOPS = 4 * 2 * K * N * S

F32 = mybir.dt.float32
BF16 = mybir.dt.bfloat16
I32 = mybir.dt.int32
U32 = mybir.dt.uint32
U16 = mybir.dt.uint16
U8 = mybir.dt.uint8
FP8X4 = mybir.dt.float8_e4m3fn_x4
FP4X4 = mybir.dt.float4_e2m1fn_x4
ACT = mybir.ActivationFunctionType
ALU = mybir.AluOpType

P = 128
BANK = 512


def tile_moe_experts_write_with_weights_kernel(
    tc, xt, wa_words, wa_scales, va_words, va_scales, wb_words, wb_scales, vb_words, vb_scales, pr, old, offs, offs2, out
):
    nc = tc.nc
    with ExitStack() as ctx:
        sb = ctx.enter_context(tc.tile_pool(name="sb", bufs=1))
        ps = ctx.enter_context(tc.psum_pool(name="ps", bufs=1))
        bank = [ps.tile([P, BANK], F32, name=f"bank{i}") for i in range(8)]

        planes = sb.tile([P, 4 * N], U8, name="planes", align_bytes=64)
        nc.vector.memset(planes[:].bitcast(I32), 0)

        def load_scales(slot, scales):
            rows = scales[0].bitcast(I32)
            for q in range(4):
                nc.sync.dma_start(
                    out=planes[32 * q : 32 * q + 4, slot * N : (slot + 1) * N].bitcast(I32), in_=rows[4 * q : 4 * q + 4, :]
                )

        def load_words(name, words, width):
            tile = sb.tile([P, width], U8, name=name, align_bytes=64)
            nc.sync.dma_start(out=tile[:].bitcast(I32), in_=words.bitcast(I32))
            return tile

        list_a = sb.tile([P, S // 16], U16, name="list_a")
        list_b = sb.tile([P, S // 16], U16, name="list_b")
        rows_of = xt.rearrange("(p j) t -> p j t", j=4)
        raw = {}
        for pair in range(2):
            for half in range(2):
                raw[pair, half] = sb.tile([P, 2, T // 2], F32, name=f"raw{pair}{half}")
                nc.sync.dma_start(
                    out=raw[pair, half][:], in_=rows_of[:, 2 * pair : 2 * pair + 2, half * (T // 2) : (half + 1) * (T // 2)]
                )
            if pair == 0:
                nc.sync.dma_start(list_a[:], offs)
        va = load_words("va", va_words[0], 2 * N)
        load_scales(0, va_scales)
        nc.sync.dma_start(list_b[:], offs2)
        wa = load_words("wa", wa_words[0].rearrange("p n r -> p (n r)"), 4 * N)
        load_scales(2, wa_scales)
        vb = load_words("vb", vb_words[0], 2 * N)
        load_scales(1, vb_scales)
        wb = load_words("wb", wb_words[0].rearrange("p n r -> p (n r)"), 4 * N)
        load_scales(3, wb_scales)
        prior = sb.tile([P, 2, T], F32, name="prior")
        state = sb.tile([P, 2, T], F32, name="state")
        nc.sync.dma_start(out=prior[:], in_=pr.rearrange("(h p) t -> p h t", p=P))
        nc.sync.dma_start(out=state[:], in_=old.rearrange("(h p) t -> p h t", p=P))

        ident = sb.tile([P, P], F32, name="ident")
        make_identity(nc, ident[:])

        pairs = [sb.tile([P, T], U32, name=f"pairs{i}") for i in range(2)]

        def cast(pair, half, copy, lo=0, hi=T // 2):
            first = half * (T // 2)
            copy(
                out=pairs[pair][:, first + lo : first + hi].bitcast(BF16).rearrange("p (t j) -> p t j", j=2),
                in_=raw[pair, half][:, :, lo:hi].rearrange("p j t -> p t j"),
            )

        stage = sb.tile([P, 2 * S], U32, name="stage", align_bytes=64)
        picked_a = sb.tile([P, 2 * S], U32, name="picked_a")
        grouped_b = sb.tile([P, 2 * S], U32, name="grouped_b", align_bytes=64)
        picked = [picked_a[:], stage[:]]
        woven = [stage[:], grouped_b[:]]
        lists = [list_a, list_b]

        def gather(e, pair):
            nc.vector.tensor_copy(picked[e][:, pair * S : (pair + 1) * S], pairs[pair][:].indirect(lists[e][:]))

        def quantise(e):
            nc.vector.tensor_copy(
                out=woven[e].bitcast(I32).rearrange("p (c w) -> p c w", w=2),
                in_=picked[e].bitcast(I32).rearrange("p (w c) -> p c w", w=2),
            )
            codes = sb.tile([P, S], U32, name=f"codes{e}", align_bytes=64)
            scale = sb.tile([P, S], U8, name=f"scale{e}", align_bytes=64)
            nc.vector.quantize_mx(out=codes[:].bitcast(FP8X4), scales=scale[:], in_=woven[e].bitcast(BF16))
            return codes, scale

        def product(acc, words, dtype, slot, h, tokens):
            width = P * (2 if dtype == FP4X4 else 4)
            nc.tensor.matmul_mx(
                out=acc[:],
                lhsT=words[:, h * width : (h + 1) * width].bitcast(dtype),
                lhsT_scale=planes[:, slot * N + h * P : slot * N + (h + 1) * P],
                rhs=tokens[0][:].bitcast(FP8X4),
                rhs_scale=tokens[1][:],
                start=True,
                stop=True,
            )

        def turn(bank_tile, at, src, start, stop):
            blocks = src.shape[1] // P
            for j in range(blocks):
                nc.tensor.matmul(
                    bank_tile[:, at + j * P : at + (j + 1) * P],
                    lhsT=src[:, j * P : (j + 1) * P],
                    rhs=ident[:],
                    start=start and j == 0,
                    stop=stop and j == blocks - 1,
                    is_transpose=True,
                )

        def turn_wide(banks, src, start, stop):
            for i, lo in enumerate(range(0, src.shape[1], BANK)):
                turn(banks[i], 0, src[:, lo : min(lo + BANK, src.shape[1])], start, stop)

        tiny = 2.0**-64
        gates = sb.tile([P, 5 * S], F32, name="gates")
        logs = sb.tile([P, 5 * S], F32, name="logs")
        log_a0 = sb.tile([P, S], F32, name="log_a0")

        def softplus(w, acc, log):
            nc.vector.scalar_tensor_tensor(w, log, -1.0, acc[:], ALU.mult, ALU.max)
            return w

        def evacuate(v, acc):
            nc.scalar.copy(v, acc[:])
            return v

        share = 352
        cast(0, 0, nc.scalar.copy)
        cast(0, 1, nc.vector.tensor_copy)
        gather(0, 0)
        cast(1, 0, nc.scalar.copy)
        cast(1, 1, nc.vector.tensor_copy, 0, share)
        cast(1, 1, nc.scalar.copy, share, T // 2)
        gather(0, 1)
        tok_a = quantise(0)
        for h in range(2):
            product(bank[h], va, FP4X4, 0, h, tok_a)
        spread = gates[:, : 4 * S].rearrange("p (a b) -> p a b", a=4)[:, :, :P]
        nc.scalar.activation(spread, bank[0][:].rearrange("p (a b) -> p a b", a=4), ACT.Sigmoid, scale=-1.0)
        nc.scalar.activation(log_a0[:].rearrange("p (a b) -> p a b", a=4), spread, ACT.Ln, bias=tiny)
        gather(1, 0)
        gather(1, 1)
        tok_b = quantise(1)
        for h in range(2):
            product(bank[3 + h], vb, FP4X4, 1, h, tok_b)
        product(bank[2], wa, FP8X4, 2, 0, tok_a)
        product(bank[6], wa, FP8X4, 2, 1, tok_a)
        product(bank[5], wb, FP8X4, 3, 0, tok_b)
        product(bank[7], wb, FP8X4, 3, 1, tok_b)

        win = {}
        for name in ("a0", "a1", "a2", "b0", "b1"):
            win[name] = sb.tile([P, T], F32, name=f"win_{name}")
            (nc.vector if name in ("a0", "a1", "a2") else nc.gpsimd).memset(win[name][:], 0.0)

        sa0_tile = sb.tile([P, S], F32, name="sa0", tag="sa0")
        sa0 = softplus(sa0_tile[:], bank[0], log_a0[:])
        nc.vector.tensor_copy(win["a0"][:].indirect(list_a[:]), sa0)
        a0 = evacuate(gates[:, 3 * S : 4 * S], bank[2])
        nc.vector.tensor_tensor(win["a1"][:].indirect(list_a[:]), sa0, a0, ALU.mult)

        kept = sb.tile([P, 2, T], F32, name="kept", tag="sa0")
        for h in range(2):
            for i in range(2):
                cols = slice(i * BANK, (i + 1) * BANK)
                nc.gpsimd.tensor_tensor(kept[:, h, cols], prior[:, h, cols], state[:, h, cols], ALU.mult)

        for slot, acc in ((1, bank[1]), (0, bank[3]), (2, bank[4])):
            nc.scalar.activation(gates[:, slot * S : (slot + 1) * S], acc[:], ACT.Sigmoid, scale=-1.0)
        lo, hi = S - 64, 2 * S + 64
        nc.scalar.activation(logs[:, lo:hi], gates[:, lo:hi], ACT.Ln, bias=tiny)
        nc.scalar.activation(
            logs[:, : 2 * hi].rearrange("p (a b) -> p a b", a=2)[:, :, :lo],
            gates[:, : 2 * hi].rearrange("p (a b) -> p a b", a=2)[:, :, :lo],
            ACT.Ln,
            bias=tiny,
        )
        sa1 = softplus(a0, bank[1], logs[:, S : 2 * S])
        nc.vector.tensor_copy(win["a2"][:].indirect(list_a[:]), sa1)
        b0 = evacuate(logs[:, S : 2 * S], bank[5])
        a1 = evacuate(gates[:, :S], bank[6])
        b1 = evacuate(gates[:, 2 * S : 3 * S], bank[7])
        weights_b = sb.tile([P, 2, S], F32, name="weights_b")
        sb0 = softplus(weights_b[:, 0, :], bank[3], logs[:, :S])
        sb1 = softplus(weights_b[:, 1, :], bank[4], logs[:, 2 * S : 3 * S])
        pa1 = sb.tile([P, S], F32, name="pa1")
        pb1 = sb.tile([P, S], F32, name="pb1")
        nc.gpsimd.tensor_tensor(pa1[:], sa1, a1, ALU.mult)
        nc.gpsimd.tensor_tensor(pb1[:], sb1, b1, ALU.mult)
        nc.vector.tensor_copy(win["b0"][:].indirect(list_b[:]), sb0)
        nc.vector.tensor_copy(win["b1"][:].indirect(list_b[:]), sb1)

        den0, den1 = [bank[1], bank[5]], [bank[6], bank[7]]
        last = T - P
        turn_wide(den0, win["a0"][:], True, False)
        turn_wide(den0, prior[:, 0, :], False, False)
        turn_wide(den1, prior[:, 1, :], True, False)
        turn_wide(den1, win["a2"][:, :last], False, False)
        turn_wide(den0, win["b0"][:], False, True)
        turn(den1[0], 0, win["b1"][:, :BANK], False, True)
        turn(den1[1], 0, win["b1"][:, BANK:], False, False)
        turn(den1[1], BANK - P, win["a2"][:, last:], False, True)
        lo, hi = BANK - 64, 3 * BANK + 64
        log_den = sb.tile([P, 2 * hi], F32, name="log_den")
        inv = sb.tile([P, 2 * hi], F32, name="inv")
        for slot, acc in ((1, den0[0]), (2, den0[1]), (0, den1[0]), (3, den1[1])):
            nc.scalar.activation(log_den[:, slot * BANK : (slot + 1) * BANK], acc[:], ACT.Ln)

        num0 = [bank[3], bank[4]]
        turn_wide(num0, win["a1"][:], True, False)
        turn_wide(num0, kept[:, 0, :], False, False)
        nc.vector.tensor_tensor(win["b0"][:].indirect(list_b[:]), sb0, b0, ALU.mult)
        turn_wide(num0, win["b0"][:], False, True)
        nc.vector.tensor_copy(win["b1"][:].indirect(list_b[:]), pb1[:])
        nc.vector.tensor_copy(win["a2"][:].indirect(list_a[:]), pa1[:])

        nc.scalar.activation(inv[:, lo:hi], log_den[:, lo:hi], ACT.Exp, scale=-1.0)
        num0_t = log_den[:, BANK : 3 * BANK]
        inv0_t = inv[:, BANK : 3 * BANK]
        y0t = sb.tile([P, T], F32, name="y0t")
        halves = [slice(0, BANK), slice(BANK, T)]
        nc.scalar.copy(num0_t[:, halves[0]], num0[0][:])
        nc.scalar.activation(
            inv[:].rearrange("p (a b) -> p a b", a=2)[:, :, :lo],
            log_den[:].rearrange("p (a b) -> p a b", a=2)[:, :, :lo],
            ACT.Exp,
            scale=-1.0,
        )
        nc.scalar.copy(num0_t[:, halves[1]], num0[1][:])
        for cols in halves:
            nc.gpsimd.tensor_tensor(y0t[:, cols], num0_t[:, cols], inv0_t[:, cols], ALU.mult)

        step = 256
        mine = T - step
        rest_t = [bank[0], bank[2]]
        turn_wide(rest_t, kept[:, 1, :mine], True, False)
        turn_wide(rest_t, win["b1"][:, :mine], False, True)
        inv1 = den1
        turn(inv1[0], 0, inv[:, :BANK], True, True)
        turn(inv1[1], 0, inv[:, 3 * BANK : 4 * BANK], True, True)
        rest_lo = log_den[:, :BANK]
        rest_hi = log_den[:, 3 * BANK + step : 4 * BANK]
        nc.scalar.copy(rest_lo, rest_t[0][:])
        nc.scalar.copy(rest_hi, rest_t[1][:, : mine - BANK])
        rest = den0
        turn(rest[0], 0, rest_lo, True, True)
        turn(rest[1], 0, rest_hi, True, True)
        inv_end = sb.tile([P, step], F32, name="inv_end")
        nc.scalar.copy(inv_end[:], inv1[1][:, BANK - step :])
        num1 = sb.tile([P, mine], F32, name="num1")
        rest_end = num0_t[:, :step]
        nc.gpsimd.tensor_tensor(rest_end, kept[:, 1, mine:], win["b1"][:, mine:], ALU.add)

        turn_wide(num0, y0t[:], True, True)
        y0 = sb.tile([P, T], F32, name="y0")
        for i, cols in enumerate(halves):
            nc.scalar.copy(y0[:, cols], num0[i][:])
            nc.scalar.dma_start(out=out[0:P, cols], in_=y0[:, cols])

        y1 = sb.tile([P, mine], F32, name="y1")
        num_end = num0_t[:, mine:]
        nc.gpsimd.tensor_tensor(num_end, rest_end, win["a2"][:, mine:], ALU.add)
        y1_end = y0t[:, mine:]
        nc.gpsimd.tensor_tensor(y1_end, num_end, inv_end[:], ALU.mult)
        nc.scalar.dma_start(out=out[P : 2 * P, mine:], in_=y1_end)

        def add(c):
            i, lo = divmod(c * step, BANK)
            cols = slice(c * step, (c + 1) * step)
            nc.vector.tensor_tensor(num1[:, cols], rest[i][:, lo : lo + step], win["a2"][:, cols], ALU.add)

        def finish(c):
            i, lo = divmod(c * step, BANK)
            cols = slice(c * step, (c + 1) * step)
            nc.vector.tensor_tensor(y1[:, cols], inv1[i][:, lo : lo + step], num1[:, cols], ALU.mult)
            nc.sync.dma_start(out=out[P : 2 * P, cols], in_=y1[:, cols])

        add(0)
        for c in range(1, mine // step):
            add(c)
            finish(c - 1)
        finish(mine // step - 1)
